import numpy as np
import ml_dtypes


def mxq(x, axis, fmt="e4m3"):
    dtype, down = {"e4m3": (ml_dtypes.float8_e4m3fn, 7), "e5m2": (ml_dtypes.float8_e5m2, 14)}[fmt]
    v = np.moveaxis(np.asarray(x, np.float32).astype(ml_dtypes.bfloat16).astype(np.float64), axis, -1)
    blocks = v.reshape(v.shape[:-1] + (-1, 32))
    amax = np.abs(blocks).max(-1, keepdims=True)
    byte = np.maximum(np.where(amax > 0, np.frexp(amax)[1] - 1 + 127, 0) - down, 1)
    scale = np.exp2(byte - 127.0)
    codes = (blocks / scale).astype(np.float32).astype(dtype).astype(np.float64)
    return np.moveaxis((codes * scale).reshape(v.shape), -1, axis)


WIDE = False


def mx_kscale(k):
    if not WIDE:
        return np.ones(k)
    levels = np.array([10, -10, 5, -5, 0])
    if k % 512:
        return np.exp2(np.random.permutation(np.resize(levels, k // 32))).repeat(32)
    a = np.empty((k // 512, 16))
    for p in range(k // 512):
        a[p, :8] = np.random.permutation(np.resize(levels, 8))
        for g in range(8):
            far = levels[np.abs(levels - a[p, g]) >= 10]
            a[p, g + 8] = far[np.random.randint(len(far))]
    return np.exp2(a.ravel()).repeat(32)


def f64(x):
    return np.asarray(x).astype(np.float64)


def striped(idx):
    return np.tile(idx.reshape(-1, 16).T, (8, 1)).astype(np.uint16)


def unstriped(offs):
    return offs[:16].T.reshape(-1).astype(np.int64)


def pack_weight(w):
    k, n = w.shape
    w = f64(np.asarray(w, np.float32).astype(ml_dtypes.bfloat16)).reshape(k // 32, 32, n)
    amax = np.abs(w).max(1)
    byte = np.clip(np.where(amax > 0, np.frexp(amax)[1] - 1 + 127 - 7, 1), 1, 254)
    scaled = (w * np.exp2(127.0 - byte)[:, None, :]).reshape(k, n).astype(np.float32)
    words = np.ascontiguousarray(scaled.reshape(k // 512, 128, 4, n).transpose(0, 1, 3, 2)).astype(ml_dtypes.float8_e4m3fn).view(np.uint8)
    return words, np.ascontiguousarray(byte.astype(np.uint8).reshape(k // 512, 16, n))


def unpack_weight(words, scales):
    g, p, n, _ = words.shape
    vals = np.ascontiguousarray(words).view(ml_dtypes.float8_e4m3fn).astype(np.float64) * np.repeat(np.exp2(scales.astype(np.float64) - 127.0), 8, axis=1)[..., None]
    return vals.transpose(0, 1, 3, 2).reshape(g * 512, n)


K, T, S, D, N, V = 1024, 4096, 1024, 8, 256, 128
P = 2 ** 7


def setup_inputs():
    n = np.random.standard_normal
    s = mx_kscale(K)[:, None]
    packed_xT = pack_weight(n((K, T)) * s)
    return {
        "x_words": packed_xT[0],
        "x_scales": packed_xT[1],
        "w1": (n((K, N)) / np.sqrt(K) / s).astype(np.float32),
        "bin_": (np.tile(np.tile(np.arange(D), V), (P, 1))).astype(np.float32),
        "tgt": (np.tile(np.random.uniform(0.0, 0.3, S), (P, 1))).astype(np.float32),
        "true": (np.tile(np.random.uniform(1.0, 6.0, V), (P, 1))).astype(np.float32),
        "offs": striped(np.random.permutation(T)[:S]),
    }


def reference(x_words, x_scales, w1, bin_, tgt, true, offs):
    xq = unpack_weight(x_words, x_scales)[:, unstriped(offs)]
    y = mxq(f64(w1), 0, "e4m3").T @ xq
    top = y.reshape(len(y), -1, D).max(axis=2)
    ex = np.exp(y - np.repeat(top, D, axis=1))
    tot = ex.reshape(len(ex), -1, D).sum(axis=2)
    ce = f64(tgt)[:1] * (y - (np.repeat(top + np.log(tot), D, axis=1)))
    pr = ex / np.repeat(tot, D, axis=1)
    pb = pr * f64(bin_)[:1]
    ed = pb.reshape(len(pb), -1, D).sum(axis=2)
    return -1.0 * (ce.reshape(len(ce), -1, D).sum(axis=2)) + 0.2 * (np.abs(ed - f64(true)[:1]))

@@ -1,0 +1,218 @@
+from contextlib import ExitStack
+
+import concourse.mybir as mybir
+from concourse.masks import make_identity
+
+K, T, S, D, N, V = 1024, 4096, 1024, 8, 256, 128
+FLOPS = 2 * K * S * N
+
+F32 = mybir.dt.float32
+BF16 = mybir.dt.bfloat16
+I32 = mybir.dt.int32
+U32 = mybir.dt.uint32
+U16 = mybir.dt.uint16
+U8 = mybir.dt.uint8
+FP8X4 = mybir.dt.float8_e4m3fn_x4
+ALU = mybir.AluOpType
+ACT = mybir.ActivationFunctionType
+AXIS = mybir.AxisListType
+
+P = 128
+PACK = 4
+PASSES = K // (P * PACK)
+HALVES = N // P
+BANK = 512
+GPSIMD_BINS = 3
+LINE = 4
+
+
+def tile_picked_ydfl_loss_p_kernel(
+    tc, x_words, x_scales, w1, bin_, tgt, true, offs, out
+):
+    nc = tc.nc
+    with ExitStack() as ctx:
+        keep = ctx.enter_context(tc.tile_pool(name="keep", bufs=1))
+        psum = ctx.enter_context(tc.psum_pool(name="psum", bufs=1))
+
+        def sb(name, shape, dtype, tag=""):
+            return keep.tile(shape, dtype, name=name, tag=tag or name, align_bytes=64)
+
+        offsets = keep.tile([P, S // 16], U16, name="offsets")
+        nc.sync.dma_start(offsets[:], offs)
+
+        scale_table = sb("scale_table", [P, T], U8)
+        nc.vector.memset(scale_table[:].bitcast(I32), 0)
+        for q in range(4):
+            nc.gpsimd.dma_start(
+                scale_table[32 * q : 32 * q + 4 * PASSES, :].bitcast(I32),
+                x_scales[:, 4 * q : 4 * q + 4, :].bitcast(I32),
+            )
+
+        word_table = [sb("word_table%d" % o, [P, T], U32) for o in range(PASSES)]
+        w_raw = [sb("w_raw%d" % o, [P, PACK, N], F32) for o in range(PASSES)]
+        for o in range(PASSES):
+            nc.sync.dma_start(
+                word_table[o][:].bitcast(I32),
+                x_words[o].rearrange("p c r -> p (c r)").bitcast(I32),
+            )
+            nc.sync.dma_start(
+                w_raw[o][:],
+                w1[o * P * PACK : (o + 1) * P * PACK, :].rearrange("(p j) m -> p j m", j=PACK),
+            )
+
+        tgt_col = sb("tgt_col", [P, D], F32)
+        bin_col = sb("bin_col", [P, D], F32)
+        true_col = sb("true_col", [P, 1], F32)
+        nc.scalar.dma_start(tgt_col[:], tgt[0:1, :].rearrange("o (v d) -> (o v) d", d=D))
+        nc.scalar.dma_start(bin_col[:], bin_[0:1, :].rearrange("o (v d) -> (o v) d", d=D))
+        nc.scalar.dma_start(true_col[:], true[0:1, :].rearrange("o (v d) -> (o v) d", d=1))
+
+        ident = sb("ident", [P, P], F32)
+        make_identity(nc, ident[:])
+
+        banks = [psum.tile([P, BANK], F32, name="bank%d" % b) for b in range(8)]
+
+        def turn(dst, src, start, stop):
+            nc.tensor.matmul(dst, lhsT=src, rhs=ident[:], is_transpose=True, start=start, stop=stop)
+
+        def add_turned(dst, srcs):
+            for i, src in enumerate(srcs):
+                turn(dst, src, i == 0, i == len(srcs) - 1)
+
+        neg_tgt = sb("neg_tgt", [P, D], F32)
+        nc.scalar.activation(neg_tgt[:], tgt_col[:], ACT.Copy, scale=-1.0)
+        tgt_sum = sb("tgt_sum", [P, 1], F32)
+        nc.vector.tensor_reduce(tgt_sum[:], tgt_col[:], AXIS.X, ALU.add)
+        dist = sb("dist", [P, D], F32)
+        nc.vector.tensor_scalar(dist[:], bin_col[:], true_col[:], 0.2, ALU.subtract, ALU.mult)
+        tgt_sum_row = sb("tgt_sum_row", [P, V], F32)
+        add_turned(banks[7][:, 0:V], [tgt_sum[:].to_broadcast([P, P])])
+        nc.scalar.copy(tgt_sum_row[:], banks[7][:, 0:V])
+
+        picked_scales = sb("picked_scales", [P, S], U8, "picked1")
+        nc.vector.tensor_copy(picked_scales[:], scale_table[:].indirect(offsets[:]))
+        bin_scales = sb("bin_scales", [P, S], U8)
+        nc.vector.tensor_copy(
+            bin_scales[:].rearrange("p (d vb vi) -> p vb d vi", d=D, vi=16),
+            picked_scales[:].rearrange("p (vb vi d) -> p vb d vi", d=D, vi=16),
+        )
+
+        w_codes, w_scales, bin_words = [], [], []
+        for o in range(PASSES):
+            picked = sb("picked%d" % o, [P, S], U32)
+            nc.vector.tensor_copy(picked[:], word_table[o][:].indirect(offsets[:]))
+
+            w_bf = sb("w_bf%d" % o, [P, N * PACK], BF16)
+            nc.scalar.copy(
+                w_bf[:].rearrange("p (c i j) -> p c j i", i=LINE, j=PACK),
+                w_raw[o][:].rearrange("p j (c i) -> p c j i", i=LINE),
+            )
+            codes = sb("w_codes%d" % o, [P, N], U32, "word_table1" if o == 1 else "")
+            scales = sb("w_scales%d" % o, [P, N], U8)
+            nc.vector.quantize_mx(out=codes[:].bitcast(FP8X4), scales=scales[:], in_=w_bf[:])
+            w_codes.append(codes)
+            w_scales.append(scales)
+
+            by_bin = picked[:].rearrange("p (vb vi dh dl) -> p dh vb dl vi", vi=LINE, dl=LINE, dh=D // LINE)
+            parts = []
+            for dh in range(D // LINE):
+                part = sb("bin_words%d_%d" % (o, dh), [P, LINE * V], U32)
+                nc.vector.tensor_copy(
+                    part[:].rearrange("p (dl vb vi) -> p vb dl vi", dl=LINE, vi=LINE), by_bin[:, dh]
+                )
+                parts.append(part)
+            bin_words.append(parts)
+
+            if o == 0:
+                for d in range(D):
+                    logits_pass(nc, banks, d, 0, bin_words, bin_scales, w_codes, w_scales)
+
+        running = [sb("running%d" % c, [P, N], F32) for c in range(2)]
+        ce_terms = []
+        for d in range(D):
+            logits_pass(nc, banks, d, 1, bin_words, bin_scales, w_codes, w_scales)
+            y = banks[d][:, 0:N]
+            if d < 2:
+                nc.vector.tensor_copy(running[d][:], y)
+            else:
+                nc.vector.tensor_tensor(running[d % 2][:], y, running[d % 2][:], ALU.max)
+            term = sb("ce_term%d" % d, [P, N], F32)
+            nc.scalar.activation(term[:], y, ACT.Copy, scale=neg_tgt[:, d : d + 1])
+            ce_terms.append(term)
+
+        def half(tile, h):
+            return tile[:, h * P : (h + 1) * P]
+
+        top = sb("top", [P, N], F32)
+        nc.vector.tensor_tensor(top[:], running[0][:], running[1][:], ALU.max)
+        top_term = sb("top_term", [P, N], F32)
+        nc.scalar.activation(top_term[:], top[:], ACT.Copy, scale=tgt_sum[:])
+        order = list(range(HALVES, D)) + list(range(HALVES))
+        ce_sums = [banks[h][:, N : N + V] for h in range(HALVES)]
+        for i, term in enumerate(ce_terms + [top_term]):
+            for h in range(HALVES):
+                turn(ce_sums[h], half(term, h), i == 0, i == D)
+
+        exps = []
+        for d in order:
+            z = sb("z%d" % d, [P, N], F32)
+            nc.vector.tensor_tensor(z[:], banks[d][:, 0:N], top[:], ALU.subtract)
+            ex = sb("ex%d" % d, [P, N], F32)
+            nc.scalar.activation(ex[:], z[:], ACT.Exp)
+            exps.append(ex)
+
+        totals = [banks[order[h]][:, N : N + V] for h in range(HALVES)]
+        means = [banks[order[HALVES + h]][:, N : N + V] for h in range(HALVES)]
+        for i in range(D):
+            for h in range(HALVES):
+                turn(totals[h], half(exps[i], h), i == 0, i == D - 1)
+        weighted = []
+        for i, d in enumerate(order):
+            exd = sb("exd%d" % d, [P, N], F32)
+            if i < GPSIMD_BINS:
+                nc.gpsimd.tensor_scalar(exd[:], exps[i][:], dist[:, d : d + 1], 0.0, ALU.mult, ALU.add)
+            elif i < GPSIMD_BINS + 2 or i == D - 1:
+                nc.vector.tensor_scalar(exd[:], exps[i][:], dist[:, d : d + 1], None, ALU.mult)
+            else:
+                earlier = weighted.pop(GPSIMD_BINS)
+                nc.vector.scalar_tensor_tensor(
+                    exd[:], exps[i][:], dist[:, d : d + 1], earlier[:], ALU.mult, ALU.add
+                )
+            weighted.append(exd)
+        for i, exd in enumerate(weighted):
+            for h in range(HALVES):
+                turn(means[h], half(exd, h), i == 0, i == len(weighted) - 1)
+
+        def stage(name):
+            return [sb("%s%d" % (name, h), [P, V], F32) for h in range(HALVES)]
+
+        inverse, log_total, log_term, abs_mean, err, partial, result = [
+            stage(name) for name in ("inverse", "log_total", "log_term", "abs_mean", "err", "partial", "result")
+        ]
+        for h in range(HALVES):
+            nc.vector.reciprocal(inverse[h][:], totals[h])
+        nc.scalar.activation(log_total[0][:], totals[0], ACT.Ln)
+        for h in range(HALVES):
+            nc.scalar.activation(abs_mean[h][:], means[h], ACT.Abs)
+        nc.scalar.activation(log_total[1][:], totals[1], ACT.Ln)
+        for h in range(HALVES):
+            nc.vector.tensor_tensor(err[h][:], abs_mean[h][:], inverse[h][:], ALU.mult)
+        for h in range(HALVES):
+            nc.vector.tensor_tensor(partial[h][:], ce_sums[h], err[h][:], ALU.add)
+        for h in range(HALVES):
+            nc.vector.tensor_tensor(log_term[h][:], log_total[h][:], tgt_sum_row[:], ALU.mult)
+        for h in range(HALVES):
+            nc.vector.tensor_tensor(result[h][:], partial[h][:], log_term[h][:], ALU.add)
+            nc.sync.dma_start(out[h * P : (h + 1) * P, :], result[h][:])
+
+
+def logits_pass(nc, banks, d, o, bin_words, bin_scales, w_codes, w_scales):
+    nc.tensor.matmul_mx(
+        out=banks[d][:, 0:N],
+        lhsT=bin_words[o][d // LINE][:, (d % LINE) * V : (d % LINE + 1) * V].bitcast(FP8X4),
+        lhsT_scale=bin_scales[4 * o : P, d * V : (d + 1) * V],
+        rhs=w_codes[o][:].bitcast(FP8X4),
+        rhs_scale=w_scales[o][:],
+        start=(o == 0),
+        stop=(o == PASSES - 1),
+    )

@@ -15,7 +15,6 @@ U8 = mybir.dt.uint8
 FP8X4 = mybir.dt.float8_e4m3fn_x4
 ALU = mybir.AluOpType
 ACT = mybir.ActivationFunctionType
-AXIS = mybir.AxisListType
 
 P = 128
 PACK = 4
@@ -23,6 +22,7 @@ PASSES = K // (P * PACK)
 HALVES = N // P
 BANK = 512
 GPSIMD_BINS = 3
+SCALE_ROWS = 32
 LINE = 4
 
 
@@ -41,31 +41,37 @@ def tile_picked_ydfl_loss_p_kernel(
         nc.sync.dma_start(offsets[:], offs)
 
         scale_table = sb("scale_table", [P, T], U8)
-        nc.vector.memset(scale_table[:].bitcast(I32), 0)
-        for q in range(4):
-            nc.gpsimd.dma_start(
-                scale_table[32 * q : 32 * q + 4 * PASSES, :].bitcast(I32),
-                x_scales[:, 4 * q : 4 * q + 4, :].bitcast(I32),
-            )
-
-        word_table = [sb("word_table%d" % o, [P, T], U32) for o in range(PASSES)]
-        w_raw = [sb("w_raw%d" % o, [P, PACK, N], F32) for o in range(PASSES)]
+        nc.sync.dma_start(
+            scale_table[0:SCALE_ROWS, :].bitcast(I32), x_scales.rearrange("o q c -> (o q) c").bitcast(I32)
+        )
+        nc.vector.memset(scale_table[32:64, :].bitcast(I32), 0)
+        nc.vector.memset(scale_table[64:P, :].bitcast(I32), 0)
+        bin_scales = [sb("bin_scales%d" % o, [P, S], U8) for o in range(PASSES)]
         for o in range(PASSES):
-            nc.sync.dma_start(
-                word_table[o][:].bitcast(I32),
-                x_words[o].rearrange("p c r -> p (c r)").bitcast(I32),
-            )
-            nc.sync.dma_start(
-                w_raw[o][:],
-                w1[o * P * PACK : (o + 1) * P * PACK, :].rearrange("(p j) m -> p j m", j=PACK),
-            )
+            nc.gpsimd.memset(bin_scales[o][:].bitcast(I32), 0)
 
+        def load_weights(o, tag):
+            raw = sb("w_raw%d" % o, [P, PACK, N], F32, tag)
+            nc.sync.dma_start(
+                raw[:], w1[o * P * PACK : (o + 1) * P * PACK, :].rearrange("(p j) m -> p j m", j=PACK)
+            )
+            return raw
+
+        def load_words(o):
+            table = sb("word_table%d" % o, [P, T], U32)
+            nc.sync.dma_start(table[:].bitcast(I32), x_words[o].rearrange("p c r -> p (c r)").bitcast(I32))
+            return table
+
+        word_table = [load_words(0)]
         tgt_col = sb("tgt_col", [P, D], F32)
         bin_col = sb("bin_col", [P, D], F32)
         true_col = sb("true_col", [P, 1], F32)
-        nc.scalar.dma_start(tgt_col[:], tgt[0:1, :].rearrange("o (v d) -> (o v) d", d=D))
-        nc.scalar.dma_start(bin_col[:], bin_[0:1, :].rearrange("o (v d) -> (o v) d", d=D))
-        nc.scalar.dma_start(true_col[:], true[0:1, :].rearrange("o (v d) -> (o v) d", d=1))
+        nc.sync.dma_start(tgt_col[:], tgt[0:1, :].rearrange("o (v d) -> (o v) d", d=D))
+        nc.sync.dma_start(bin_col[:], bin_[0:1, :].rearrange("o (v d) -> (o v) d", d=D))
+        nc.sync.dma_start(true_col[:], true[0:1, :].rearrange("o (v d) -> (o v) d", d=1))
+
+        w_raw = [load_weights(0, "")]
+        word_table.append(load_words(1))
 
         ident = sb("ident", [P, P], F32)
         make_identity(nc, ident[:])
@@ -80,22 +86,35 @@ def tile_picked_ydfl_loss_p_kernel(
                 turn(dst, src, i == 0, i == len(srcs) - 1)
 
         neg_tgt = sb("neg_tgt", [P, D], F32)
-        nc.scalar.activation(neg_tgt[:], tgt_col[:], ACT.Copy, scale=-1.0)
+        neg_tgt_sum = sb("neg_tgt_sum", [P, 1], F32)
+        nc.scalar.activation(neg_tgt[:], tgt_col[:], ACT.Copy, scale=-1.0, accum_out=neg_tgt_sum[:])
         tgt_sum = sb("tgt_sum", [P, 1], F32)
-        nc.vector.tensor_reduce(tgt_sum[:], tgt_col[:], AXIS.X, ALU.add)
+        nc.scalar.activation(tgt_sum[:], neg_tgt_sum[:], ACT.Copy, scale=-1.0)
         dist = sb("dist", [P, D], F32)
-        nc.vector.tensor_scalar(dist[:], bin_col[:], true_col[:], 0.2, ALU.subtract, ALU.mult)
+        nc.gpsimd.tensor_scalar(dist[:], bin_col[:], true_col[:], 0.2, ALU.subtract, ALU.mult)
         tgt_sum_row = sb("tgt_sum_row", [P, V], F32)
         add_turned(banks[7][:, 0:V], [tgt_sum[:].to_broadcast([P, P])])
         nc.scalar.copy(tgt_sum_row[:], banks[7][:, 0:V])
 
-        picked_scales = sb("picked_scales", [P, S], U8, "picked1")
+        picked_scales = sb("picked_scales", [P, S], U8, "w_raw1")
         nc.vector.tensor_copy(picked_scales[:], scale_table[:].indirect(offsets[:]))
-        bin_scales = sb("bin_scales", [P, S], U8)
+        dealt_scales = sb("dealt_scales", [P, S], U8)
         nc.vector.tensor_copy(
-            bin_scales[:].rearrange("p (d vb vi) -> p vb d vi", d=D, vi=16),
-            picked_scales[:].rearrange("p (vb vi d) -> p vb d vi", d=D, vi=16),
+            dealt_scales[:].rearrange("p (d vb vi) -> p vb d vi", d=D, vi=8),
+            picked_scales[:].rearrange("p (vb vi d) -> p vb d vi", d=D, vi=8),
         )
+
+        def place_scales(o):
+            for q in range(4):
+                row = 16 * o + 4 * q
+                nc.sync.dma_start(
+                    bin_scales[o][32 * q : 32 * q + 4, :].bitcast(I32),
+                    dealt_scales[row : row + 4, :].bitcast(I32),
+                )
+
+        place_scales(0)
+        w_raw.append(load_weights(1, "w_raw1"))
+        place_scales(1)
 
         w_codes, w_scales, bin_words = [], [], []
         for o in range(PASSES):
@@ -132,12 +151,15 @@ def tile_picked_ydfl_loss_p_kernel(
         for d in range(D):
             logits_pass(nc, banks, d, 1, bin_words, bin_scales, w_codes, w_scales)
             y = banks[d][:, 0:N]
-            if d < 2:
-                nc.vector.tensor_copy(running[d][:], y)
-            else:
-                nc.vector.tensor_tensor(running[d % 2][:], y, running[d % 2][:], ALU.max)
             term = sb("ce_term%d" % d, [P, N], F32)
-            nc.scalar.activation(term[:], y, ACT.Copy, scale=neg_tgt[:, d : d + 1])
+            if d < 2:
+                nc.scalar.copy(running[d][:], y)
+                nc.gpsimd.tensor_scalar(term[:], running[d][:], neg_tgt[:, d : d + 1], 0.0, ALU.mult, ALU.add)
+            else:
+                larger = sb("running%d" % d, [P, N], F32)
+                nc.vector.tensor_tensor(larger[:], y, running[d % 2][:], ALU.max)
+                running[d % 2] = larger
+                nc.scalar.activation(term[:], y, ACT.Copy, scale=neg_tgt[:, d : d + 1])
             ce_terms.append(term)
 
         def half(tile, h):
@@ -146,7 +168,7 @@ def tile_picked_ydfl_loss_p_kernel(
         top = sb("top", [P, N], F32)
         nc.vector.tensor_tensor(top[:], running[0][:], running[1][:], ALU.max)
         top_term = sb("top_term", [P, N], F32)
-        nc.scalar.activation(top_term[:], top[:], ACT.Copy, scale=tgt_sum[:])
+        nc.gpsimd.tensor_scalar(top_term[:], top[:], tgt_sum[:], 0.0, ALU.mult, ALU.add)
         order = list(range(HALVES, D)) + list(range(HALVES))
         ce_sums = [banks[h][:, N : N + V] for h in range(HALVES)]
         for i, term in enumerate(ce_terms + [top_term]):
@@ -195,12 +217,13 @@ def tile_picked_ydfl_loss_p_kernel(
         for h in range(HALVES):
             nc.scalar.activation(abs_mean[h][:], means[h], ACT.Abs)
         nc.scalar.activation(log_total[1][:], totals[1], ACT.Ln)
-        for h in range(HALVES):
+        nc.gpsimd.tensor_tensor(log_term[0][:], log_total[0][:], tgt_sum_row[:], ALU.mult)
+        late_first = list(reversed(range(HALVES)))
+        for h in late_first:
             nc.vector.tensor_tensor(err[h][:], abs_mean[h][:], inverse[h][:], ALU.mult)
-        for h in range(HALVES):
+        for h in late_first:
             nc.vector.tensor_tensor(partial[h][:], ce_sums[h], err[h][:], ALU.add)
-        for h in range(HALVES):
-            nc.vector.tensor_tensor(log_term[h][:], log_total[h][:], tgt_sum_row[:], ALU.mult)
+        nc.vector.tensor_tensor(log_term[1][:], log_total[1][:], tgt_sum_row[:], ALU.mult)
         for h in range(HALVES):
             nc.vector.tensor_tensor(result[h][:], partial[h][:], log_term[h][:], ALU.add)
             nc.sync.dma_start(out[h * P : (h + 1) * P, :], result[h][:])
@@ -210,7 +233,7 @@ def logits_pass(nc, banks, d, o, bin_words, bin_scales, w_codes, w_scales):
     nc.tensor.matmul_mx(
         out=banks[d][:, 0:N],
         lhsT=bin_words[o][d // LINE][:, (d % LINE) * V : (d % LINE + 1) * V].bitcast(FP8X4),
-        lhsT_scale=bin_scales[4 * o : P, d * V : (d + 1) * V],
+        lhsT_scale=bin_scales[o][:, d * V : (d + 1) * V],
         rhs=w_codes[o][:].bitcast(FP8X4),
         rhs_scale=w_scales[o][:],
         start=(o == 0),

@@ -21,7 +21,9 @@ PACK = 4
 PASSES = K // (P * PACK)
 HALVES = N // P
 BANK = 512
-GPSIMD_BINS = 3
+GPSIMD_BINS = 2
+CHAINS = 3
+DEALS = ((0, 2), (2, 4), (4, 8))
 SCALE_ROWS = 32
 LINE = 4
 
@@ -66,9 +68,9 @@ def tile_picked_ydfl_loss_p_kernel(
         tgt_col = sb("tgt_col", [P, D], F32)
         bin_col = sb("bin_col", [P, D], F32)
         true_col = sb("true_col", [P, 1], F32)
-        nc.sync.dma_start(tgt_col[:], tgt[0:1, :].rearrange("o (v d) -> (o v) d", d=D))
-        nc.sync.dma_start(bin_col[:], bin_[0:1, :].rearrange("o (v d) -> (o v) d", d=D))
-        nc.sync.dma_start(true_col[:], true[0:1, :].rearrange("o (v d) -> (o v) d", d=1))
+        nc.scalar.dma_start(tgt_col[:], tgt[0:1, :].rearrange("o (v d) -> (o v) d", d=D))
+        nc.scalar.dma_start(bin_col[:], bin_[0:1, :].rearrange("o (v d) -> (o v) d", d=D))
+        nc.scalar.dma_start(true_col[:], true[0:1, :].rearrange("o (v d) -> (o v) d", d=1))
 
         w_raw = [load_weights(0, "")]
         word_table.append(load_words(1))
@@ -132,41 +134,48 @@ def tile_picked_ydfl_loss_p_kernel(
             w_codes.append(codes)
             w_scales.append(scales)
 
-            by_bin = picked[:].rearrange("p (vb vi dh dl) -> p dh vb dl vi", vi=LINE, dl=LINE, dh=D // LINE)
+            by_bin = picked[:].rearrange("p (vb vi d) -> p vb d vi", vi=LINE, d=D)
             parts = []
-            for dh in range(D // LINE):
-                part = sb("bin_words%d_%d" % (o, dh), [P, LINE * V], U32)
+            for first, last in DEALS:
+                part = sb("bin_words%d_%d" % (o, first), [P, last - first, V], U32)
                 nc.vector.tensor_copy(
-                    part[:].rearrange("p (dl vb vi) -> p vb dl vi", dl=LINE, vi=LINE), by_bin[:, dh]
+                    part[:].rearrange("p d (vb vi) -> p vb d vi", vi=LINE), by_bin[:, :, first:last, :]
                 )
-                parts.append(part)
+                parts.extend(part[:, d, :] for d in range(last - first))
             bin_words.append(parts)
 
             if o == 0:
                 for d in range(D):
                     logits_pass(nc, banks, d, 0, bin_words, bin_scales, w_codes, w_scales)
 
-        running = [sb("running%d" % c, [P, N], F32) for c in range(2)]
+        def half(tile, h):
+            return tile[:, h * P : (h + 1) * P]
+
+        running = [sb("running%d" % c, [P, N], F32) for c in range(CHAINS)]
         ce_terms = []
         for d in range(D):
             logits_pass(nc, banks, d, 1, bin_words, bin_scales, w_codes, w_scales)
             y = banks[d][:, 0:N]
             term = sb("ce_term%d" % d, [P, N], F32)
-            if d < 2:
+            if d < CHAINS - 1:
                 nc.scalar.copy(running[d][:], y)
                 nc.gpsimd.tensor_scalar(term[:], running[d][:], neg_tgt[:, d : d + 1], 0.0, ALU.mult, ALU.add)
             else:
-                larger = sb("running%d" % d, [P, N], F32)
-                nc.vector.tensor_tensor(larger[:], y, running[d % 2][:], ALU.max)
-                running[d % 2] = larger
+                if d < CHAINS:
+                    nc.vector.tensor_copy(running[d][:], y)
+                else:
+                    larger = sb("running%d" % d, [P, N], F32)
+                    nc.vector.tensor_tensor(larger[:], y, running[d % CHAINS][:], ALU.max)
+                    running[d % CHAINS] = larger
                 nc.scalar.activation(term[:], y, ACT.Copy, scale=neg_tgt[:, d : d + 1])
             ce_terms.append(term)
 
-        def half(tile, h):
-            return tile[:, h * P : (h + 1) * P]
-
+        joined = sb("joined", [P, N], F32)
         top = sb("top", [P, N], F32)
-        nc.vector.tensor_tensor(top[:], running[0][:], running[1][:], ALU.max)
+        for h in range(HALVES):
+            nc.vector.tensor_tensor(half(joined, h), half(running[0], h), half(running[2], h), ALU.max)
+        for h in range(HALVES):
+            nc.vector.tensor_tensor(half(top, h), half(joined, h), half(running[1], h), ALU.max)
         top_term = sb("top_term", [P, N], F32)
         nc.gpsimd.tensor_scalar(top_term[:], top[:], tgt_sum[:], 0.0, ALU.mult, ALU.add)
         order = list(range(HALVES, D)) + list(range(HALVES))
@@ -178,7 +187,11 @@ def tile_picked_ydfl_loss_p_kernel(
         exps = []
         for d in order:
             z = sb("z%d" % d, [P, N], F32)
-            nc.vector.tensor_tensor(z[:], banks[d][:, 0:N], top[:], ALU.subtract)
+            if d == order[0]:
+                for h in range(HALVES):
+                    nc.vector.tensor_tensor(half(z, h), half(banks[d], h), half(top, h), ALU.subtract)
+            else:
+                nc.vector.tensor_tensor(z[:], banks[d][:, 0:N], top[:], ALU.subtract)
             ex = sb("ex%d" % d, [P, N], F32)
             nc.scalar.activation(ex[:], z[:], ACT.Exp)
             exps.append(ex)
@@ -193,7 +206,9 @@ def tile_picked_ydfl_loss_p_kernel(
             exd = sb("exd%d" % d, [P, N], F32)
             if i < GPSIMD_BINS:
                 nc.gpsimd.tensor_scalar(exd[:], exps[i][:], dist[:, d : d + 1], 0.0, ALU.mult, ALU.add)
-            elif i < GPSIMD_BINS + 2 or i == D - 1:
+            elif i == D - 1:
+                nc.scalar.activation(exd[:], exps[i][:], ACT.Copy, scale=dist[:, d : d + 1])
+            elif i < GPSIMD_BINS + 2 or i == D - 2:
                 nc.vector.tensor_scalar(exd[:], exps[i][:], dist[:, d : d + 1], None, ALU.mult)
             else:
                 earlier = weighted.pop(GPSIMD_BINS)
@@ -217,11 +232,10 @@ def tile_picked_ydfl_loss_p_kernel(
         for h in range(HALVES):
             nc.scalar.activation(abs_mean[h][:], means[h], ACT.Abs)
         nc.scalar.activation(log_total[1][:], totals[1], ACT.Ln)
-        nc.gpsimd.tensor_tensor(log_term[0][:], log_total[0][:], tgt_sum_row[:], ALU.mult)
-        late_first = list(reversed(range(HALVES)))
-        for h in late_first:
+        for h in range(HALVES):
             nc.vector.tensor_tensor(err[h][:], abs_mean[h][:], inverse[h][:], ALU.mult)
-        for h in late_first:
+        nc.vector.tensor_tensor(log_term[0][:], log_total[0][:], tgt_sum_row[:], ALU.mult)
+        for h in range(HALVES):
             nc.vector.tensor_tensor(partial[h][:], ce_sums[h], err[h][:], ALU.add)
         nc.vector.tensor_tensor(log_term[1][:], log_total[1][:], tgt_sum_row[:], ALU.mult)
         for h in range(HALVES):
@@ -232,7 +246,7 @@ def tile_picked_ydfl_loss_p_kernel(
 def logits_pass(nc, banks, d, o, bin_words, bin_scales, w_codes, w_scales):
     nc.tensor.matmul_mx(
         out=banks[d][:, 0:N],
-        lhsT=bin_words[o][d // LINE][:, (d % LINE) * V : (d % LINE + 1) * V].bitcast(FP8X4),
+        lhsT=bin_words[o][d].bitcast(FP8X4),
         lhsT_scale=bin_scales[o][:, d * V : (d + 1) * V],
         rhs=w_codes[o][:].bitcast(FP8X4),
         rhs_scale=w_scales[o][:],

from contextlib import ExitStack

import concourse.mybir as mybir
from concourse.masks import make_identity

K, T, S, D, N, V = 1024, 4096, 1024, 8, 256, 128
FLOPS = 2 * K * S * N

F32 = mybir.dt.float32
BF16 = mybir.dt.bfloat16
I32 = mybir.dt.int32
U32 = mybir.dt.uint32
U16 = mybir.dt.uint16
U8 = mybir.dt.uint8
FP8X4 = mybir.dt.float8_e4m3fn_x4
ALU = mybir.AluOpType
ACT = mybir.ActivationFunctionType

P = 128
PACK = 4
PASSES = K // (P * PACK)
HALVES = N // P
BANK = 512
GPSIMD_BINS = 2
CHAINS = 3
DEALS = ((0, 2), (2, 4), (4, 8))
SCALE_ROWS = 32
LINE = 4


def tile_picked_ydfl_loss_p_kernel(
    tc, x_words, x_scales, w1, bin_, tgt, true, offs, out
):
    nc = tc.nc
    with ExitStack() as ctx:
        keep = ctx.enter_context(tc.tile_pool(name="keep", bufs=1))
        psum = ctx.enter_context(tc.psum_pool(name="psum", bufs=1))

        def sb(name, shape, dtype, tag=""):
            return keep.tile(shape, dtype, name=name, tag=tag or name, align_bytes=64)

        offsets = keep.tile([P, S // 16], U16, name="offsets")
        nc.sync.dma_start(offsets[:], offs)

        scale_table = sb("scale_table", [P, T], U8)
        nc.sync.dma_start(
            scale_table[0:SCALE_ROWS, :].bitcast(I32), x_scales.rearrange("o q c -> (o q) c").bitcast(I32)
        )
        nc.vector.memset(scale_table[32:64, :].bitcast(I32), 0)
        nc.vector.memset(scale_table[64:P, :].bitcast(I32), 0)
        bin_scales = [sb("bin_scales%d" % o, [P, S], U8) for o in range(PASSES)]
        for o in range(PASSES):
            nc.gpsimd.memset(bin_scales[o][:].bitcast(I32), 0)

        def load_weights(o, tag):
            raw = sb("w_raw%d" % o, [P, PACK, N], F32, tag)
            nc.sync.dma_start(
                raw[:], w1[o * P * PACK : (o + 1) * P * PACK, :].rearrange("(p j) m -> p j m", j=PACK)
            )
            return raw

        def load_words(o):
            table = sb("word_table%d" % o, [P, T], U32)
            nc.sync.dma_start(table[:].bitcast(I32), x_words[o].rearrange("p c r -> p (c r)").bitcast(I32))
            return table

        word_table = [load_words(0)]
        tgt_col = sb("tgt_col", [P, D], F32)
        bin_col = sb("bin_col", [P, D], F32)
        true_col = sb("true_col", [P, 1], F32)
        nc.scalar.dma_start(tgt_col[:], tgt[0:1, :].rearrange("o (v d) -> (o v) d", d=D))
        nc.scalar.dma_start(bin_col[:], bin_[0:1, :].rearrange("o (v d) -> (o v) d", d=D))
        nc.scalar.dma_start(true_col[:], true[0:1, :].rearrange("o (v d) -> (o v) d", d=1))

        w_raw = [load_weights(0, "")]
        word_table.append(load_words(1))

        ident = sb("ident", [P, P], F32)
        make_identity(nc, ident[:])

        banks = [psum.tile([P, BANK], F32, name="bank%d" % b) for b in range(8)]

        def turn(dst, src, start, stop):
            nc.tensor.matmul(dst, lhsT=src, rhs=ident[:], is_transpose=True, start=start, stop=stop)

        def add_turned(dst, srcs):
            for i, src in enumerate(srcs):
                turn(dst, src, i == 0, i == len(srcs) - 1)

        neg_tgt = sb("neg_tgt", [P, D], F32)
        neg_tgt_sum = sb("neg_tgt_sum", [P, 1], F32)
        nc.scalar.activation(neg_tgt[:], tgt_col[:], ACT.Copy, scale=-1.0, accum_out=neg_tgt_sum[:])
        tgt_sum = sb("tgt_sum", [P, 1], F32)
        nc.scalar.activation(tgt_sum[:], neg_tgt_sum[:], ACT.Copy, scale=-1.0)
        dist = sb("dist", [P, D], F32)
        nc.gpsimd.tensor_scalar(dist[:], bin_col[:], true_col[:], 0.2, ALU.subtract, ALU.mult)
        tgt_sum_row = sb("tgt_sum_row", [P, V], F32)
        add_turned(banks[7][:, 0:V], [tgt_sum[:].to_broadcast([P, P])])
        nc.scalar.copy(tgt_sum_row[:], banks[7][:, 0:V])

        picked_scales = sb("picked_scales", [P, S], U8, "w_raw1")
        nc.vector.tensor_copy(picked_scales[:], scale_table[:].indirect(offsets[:]))
        dealt_scales = sb("dealt_scales", [P, S], U8)
        nc.vector.tensor_copy(
            dealt_scales[:].rearrange("p (d vb vi) -> p vb d vi", d=D, vi=8),
            picked_scales[:].rearrange("p (vb vi d) -> p vb d vi", d=D, vi=8),
        )

        def place_scales(o):
            for q in range(4):
                row = 16 * o + 4 * q
                nc.sync.dma_start(
                    bin_scales[o][32 * q : 32 * q + 4, :].bitcast(I32),
                    dealt_scales[row : row + 4, :].bitcast(I32),
                )

        place_scales(0)
        w_raw.append(load_weights(1, "w_raw1"))
        place_scales(1)

        w_codes, w_scales, bin_words = [], [], []
        for o in range(PASSES):
            picked = sb("picked%d" % o, [P, S], U32)
            nc.vector.tensor_copy(picked[:], word_table[o][:].indirect(offsets[:]))

            w_bf = sb("w_bf%d" % o, [P, N * PACK], BF16)
            nc.scalar.copy(
                w_bf[:].rearrange("p (c i j) -> p c j i", i=LINE, j=PACK),
                w_raw[o][:].rearrange("p j (c i) -> p c j i", i=LINE),
            )
            codes = sb("w_codes%d" % o, [P, N], U32, "word_table1" if o == 1 else "")
            scales = sb("w_scales%d" % o, [P, N], U8)
            nc.vector.quantize_mx(out=codes[:].bitcast(FP8X4), scales=scales[:], in_=w_bf[:])
            w_codes.append(codes)
            w_scales.append(scales)

            by_bin = picked[:].rearrange("p (vb vi d) -> p vb d vi", vi=LINE, d=D)
            parts = []
            for first, last in DEALS:
                part = sb("bin_words%d_%d" % (o, first), [P, last - first, V], U32)
                nc.vector.tensor_copy(
                    part[:].rearrange("p d (vb vi) -> p vb d vi", vi=LINE), by_bin[:, :, first:last, :]
                )
                parts.extend(part[:, d, :] for d in range(last - first))
            bin_words.append(parts)

            if o == 0:
                for d in range(D):
                    logits_pass(nc, banks, d, 0, bin_words, bin_scales, w_codes, w_scales)

        def half(tile, h):
            return tile[:, h * P : (h + 1) * P]

        running = [sb("running%d" % c, [P, N], F32) for c in range(CHAINS)]
        ce_terms = []
        for d in range(D):
            logits_pass(nc, banks, d, 1, bin_words, bin_scales, w_codes, w_scales)
            y = banks[d][:, 0:N]
            term = sb("ce_term%d" % d, [P, N], F32)
            if d < CHAINS - 1:
                nc.scalar.copy(running[d][:], y)
                nc.gpsimd.tensor_scalar(term[:], running[d][:], neg_tgt[:, d : d + 1], 0.0, ALU.mult, ALU.add)
            else:
                if d < CHAINS:
                    nc.vector.tensor_copy(running[d][:], y)
                else:
                    larger = sb("running%d" % d, [P, N], F32)
                    nc.vector.tensor_tensor(larger[:], y, running[d % CHAINS][:], ALU.max)
                    running[d % CHAINS] = larger
                nc.scalar.activation(term[:], y, ACT.Copy, scale=neg_tgt[:, d : d + 1])
            ce_terms.append(term)

        joined = sb("joined", [P, N], F32)
        top = sb("top", [P, N], F32)
        for h in range(HALVES):
            nc.vector.tensor_tensor(half(joined, h), half(running[0], h), half(running[2], h), ALU.max)
        for h in range(HALVES):
            nc.vector.tensor_tensor(half(top, h), half(joined, h), half(running[1], h), ALU.max)
        top_term = sb("top_term", [P, N], F32)
        nc.gpsimd.tensor_scalar(top_term[:], top[:], tgt_sum[:], 0.0, ALU.mult, ALU.add)
        order = list(range(HALVES, D)) + list(range(HALVES))
        ce_sums = [banks[h][:, N : N + V] for h in range(HALVES)]
        for i, term in enumerate(ce_terms + [top_term]):
            for h in range(HALVES):
                turn(ce_sums[h], half(term, h), i == 0, i == D)

        exps = []
        for d in order:
            z = sb("z%d" % d, [P, N], F32)
            if d == order[0]:
                for h in range(HALVES):
                    nc.vector.tensor_tensor(half(z, h), half(banks[d], h), half(top, h), ALU.subtract)
            else:
                nc.vector.tensor_tensor(z[:], banks[d][:, 0:N], top[:], ALU.subtract)
            ex = sb("ex%d" % d, [P, N], F32)
            nc.scalar.activation(ex[:], z[:], ACT.Exp)
            exps.append(ex)

        totals = [banks[order[h]][:, N : N + V] for h in range(HALVES)]
        means = [banks[order[HALVES + h]][:, N : N + V] for h in range(HALVES)]
        for i in range(D):
            for h in range(HALVES):
                turn(totals[h], half(exps[i], h), i == 0, i == D - 1)
        weighted = []
        for i, d in enumerate(order):
            exd = sb("exd%d" % d, [P, N], F32)
            if i < GPSIMD_BINS:
                nc.gpsimd.tensor_scalar(exd[:], exps[i][:], dist[:, d : d + 1], 0.0, ALU.mult, ALU.add)
            elif i == D - 1:
                nc.scalar.activation(exd[:], exps[i][:], ACT.Copy, scale=dist[:, d : d + 1])
            elif i < GPSIMD_BINS + 2 or i == D - 2:
                nc.vector.tensor_scalar(exd[:], exps[i][:], dist[:, d : d + 1], None, ALU.mult)
            else:
                earlier = weighted.pop(GPSIMD_BINS)
                nc.vector.scalar_tensor_tensor(
                    exd[:], exps[i][:], dist[:, d : d + 1], earlier[:], ALU.mult, ALU.add
                )
            weighted.append(exd)
        for i, exd in enumerate(weighted):
            for h in range(HALVES):
                turn(means[h], half(exd, h), i == 0, i == len(weighted) - 1)

        def stage(name):
            return [sb("%s%d" % (name, h), [P, V], F32) for h in range(HALVES)]

        inverse, log_total, log_term, abs_mean, err, partial, result = [
            stage(name) for name in ("inverse", "log_total", "log_term", "abs_mean", "err", "partial", "result")
        ]
        for h in range(HALVES):
            nc.vector.reciprocal(inverse[h][:], totals[h])
        nc.scalar.activation(log_total[0][:], totals[0], ACT.Ln)
        for h in range(HALVES):
            nc.scalar.activation(abs_mean[h][:], means[h], ACT.Abs)
        nc.scalar.activation(log_total[1][:], totals[1], ACT.Ln)
        for h in range(HALVES):
            nc.vector.tensor_tensor(err[h][:], abs_mean[h][:], inverse[h][:], ALU.mult)
        nc.vector.tensor_tensor(log_term[0][:], log_total[0][:], tgt_sum_row[:], ALU.mult)
        for h in range(HALVES):
            nc.vector.tensor_tensor(partial[h][:], ce_sums[h], err[h][:], ALU.add)
        nc.vector.tensor_tensor(log_term[1][:], log_total[1][:], tgt_sum_row[:], ALU.mult)
        for h in range(HALVES):
            nc.vector.tensor_tensor(result[h][:], partial[h][:], log_term[h][:], ALU.add)
            nc.sync.dma_start(out[h * P : (h + 1) * P, :], result[h][:])


def logits_pass(nc, banks, d, o, bin_words, bin_scales, w_codes, w_scales):
    nc.tensor.matmul_mx(
        out=banks[d][:, 0:N],
        lhsT=bin_words[o][d].bitcast(FP8X4),
        lhsT_scale=bin_scales[o][:, d * V : (d + 1) * V],
        rhs=w_codes[o][:].bitcast(FP8X4),
        rhs_scale=w_scales[o][:],
        start=(o == 0),
        stop=(o == PASSES - 1),
    )
